import numpy as np
import ml_dtypes


def mxq(x, axis, fmt="e4m3"):
    dtype, down = {"e4m3": (ml_dtypes.float8_e4m3fn, 7), "e5m2": (ml_dtypes.float8_e5m2, 14)}[fmt]
    v = np.moveaxis(np.asarray(x, np.float32).astype(ml_dtypes.bfloat16).astype(np.float64), axis, -1)
    blocks = v.reshape(v.shape[:-1] + (-1, 32))
    amax = np.abs(blocks).max(-1, keepdims=True)
    byte = np.maximum(np.where(amax > 0, np.frexp(amax)[1] - 1 + 127, 0) - down, 1)
    scale = np.exp2(byte - 127.0)
    codes = (blocks / scale).astype(np.float32).astype(dtype).astype(np.float64)
    return np.moveaxis((codes * scale).reshape(v.shape), -1, axis)


WIDE = False


def mx_kscale(k):
    if not WIDE:
        return np.ones(k)
    levels = np.array([10, -10, 5, -5, 0])
    if k % 512:
        return np.exp2(np.random.permutation(np.resize(levels, k // 32))).repeat(32)
    a = np.empty((k // 512, 16))
    for p in range(k // 512):
        a[p, :8] = np.random.permutation(np.resize(levels, 8))
        for g in range(8):
            far = levels[np.abs(levels - a[p, g]) >= 10]
            a[p, g + 8] = far[np.random.randint(len(far))]
    return np.exp2(a.ravel()).repeat(32)


def f64(x):
    return np.asarray(x).astype(np.float64)


E2M1 = np.array([0.0, 0.5, 1.0, 1.5, 2.0, 3.0, 4.0, 6.0, -0.0, -0.5, -1.0, -1.5, -2.0, -3.0, -4.0, -6.0])


def pack_weight(w, fmt):
    k, n = w.shape
    w = f64(np.asarray(w, np.float32).astype(ml_dtypes.bfloat16)).reshape(k // 32, 32, n)
    amax = np.abs(w).max(1)
    if fmt == "e4m3":
        byte = np.frexp(amax)[1] - 1 + 127 - 7
    else:
        mant, ex = np.frexp(amax / 6.0)
        byte = np.where(mant > 0.5, ex, ex - 1) + 127
    byte = np.clip(np.where(amax > 0, byte, 1), 1, 254)
    scaled = (w * np.exp2(127.0 - byte)[:, None, :]).reshape(k, n).astype(np.float32)
    by_word = np.ascontiguousarray(scaled.reshape(k // 512, 128, 4, n).transpose(0, 1, 3, 2))
    if fmt == "e4m3":
        words = by_word.astype(ml_dtypes.float8_e4m3fn).view(np.uint8)
    else:
        c = by_word.astype(ml_dtypes.float4_e2m1fn).view(np.uint8) & 0xF
        words = (c[..., 0::2] | (c[..., 1::2] << 4)).reshape(k // 512, 128, 2 * n)
    return np.ascontiguousarray(words), np.ascontiguousarray(byte.astype(np.uint8).reshape(k // 512, 16, n))


def unpack_weight(words, scales, fmt):
    g, _, n = scales.shape
    words = np.ascontiguousarray(words).reshape(g, 128, n, -1)
    if fmt == "e4m3":
        vals = words.view(ml_dtypes.float8_e4m3fn).astype(np.float64)
    else:
        nib = np.empty((g, 128, n, 4), np.uint8)
        nib[..., 0::2] = words & 0xF
        nib[..., 1::2] = words >> 4
        vals = E2M1[nib]
    vals = vals * np.repeat(np.exp2(scales.astype(np.float64) - 127.0), 8, axis=1)[..., None]
    return vals.transpose(0, 1, 3, 2).reshape(g * 512, n)


def planes(y):
    n, m = y.shape
    v = y.astype(np.float32).astype(ml_dtypes.bfloat16).astype(np.float64).reshape(n // 32, 32, m)
    top = np.abs(v).max(1)
    byte = np.clip(np.where(top > 0, np.frexp(top)[1] - 1 + 127 - 7, 1), 1, 254)
    codes = (v * np.exp2(127.0 - byte)[:, None, :]).reshape(n, m).astype(np.float32).astype(ml_dtypes.float8_e4m3fn).view(np.uint8)
    words = codes.reshape(n // 512, 128, 4, m).transpose(0, 1, 3, 2)
    return np.ascontiguousarray(words), np.ascontiguousarray(byte.astype(np.uint8).reshape(n // 512, 16, m))


D, K, M, T = 512, 512, 512, 1024


def setup_inputs():
    n = np.random.standard_normal
    s = mx_kscale(K)[:, None]
    p_w0 = pack_weight(n((K, M)) / np.sqrt(K) / s, "e2m1")
    p_w1 = pack_weight(n((K, M)) / np.sqrt(K) / s, "e4m3")
    return {
        "x": (n((K, T + 2 * D)) * s).astype(np.float32),
        "w0_words": p_w0[0],
        "w0_scales": p_w0[1],
        "w1_words": p_w1[0],
        "w1_scales": p_w1[1],
        "w2": (n((K, M)) / np.sqrt(K) / s).astype(np.float32),
        "b": (0.3 * n(512)).astype(np.float32),
    }


def reference(x, w0_words, w0_scales, w1_words, w1_scales, w2, b):
    x_ = mxq(f64(x), 0, "e4m3")
    w0_ = unpack_weight(w0_words, w0_scales, "e2m1")
    w1_ = unpack_weight(w1_words, w1_scales, "e4m3")
    w2_ = mxq(f64(w2), 0, "e4m3")
    y = w0_.T @ x_[:, :T] + w1_.T @ x_[:, D:D + T] + w2_.T @ x_[:, 2 * D:]
    out_0 = y + f64(b)[:, None]
    return (out_0,) + planes(out_0)

@@ -1,0 +1,275 @@
+from contextlib import ExitStack
+
+import concourse.mybir as mybir
+
+D, K, M, T = 512, 512, 512, 1024
+FLOPS = 3 * 2 * K * M * T
+
+F32 = mybir.dt.float32
+BF16 = mybir.dt.bfloat16
+I32 = mybir.dt.int32
+U32 = mybir.dt.uint32
+U8 = mybir.dt.uint8
+FP8X4 = mybir.dt.float8_e4m3fn_x4
+FP4X4 = mybir.dt.float4_e2m1fn_x4
+ACT = mybir.ActivationFunctionType
+
+P = 128
+PACK = 4
+W = 128
+GROUPS = D // W
+CHUNKS = 4
+HALF_M = P // 2
+ORDER = (1, 2, 0, 3)
+
+
+def tile_mix_dconv_fm_pl_bias_kernel(
+    tc, x, w0_words, w0_scales, w1_words, w1_scales, w2, b, out_0, out_1, out_2
+):
+    nc = tc.nc
+    with ExitStack() as ctx:
+        sb = ctx.enter_context(tc.tile_pool(name="sb", bufs=1))
+        ps = ctx.enter_context(tc.psum_pool(name="ps", bufs=1))
+        ctx.enter_context(tc.manual_schedule())
+
+        def tile(name, shape, dtype):
+            return sb.tile(shape, dtype, name=name, align_bytes=64)
+
+        w0_raw = tile("w0_raw", [P, 2 * M], U8)
+        w0_codes = tile("w0_codes", [P, 2 * M], U8)
+        w1_raw = tile("w1_raw", [P, M], U32)
+        w1_codes = tile("w1_codes", [P, M], U32)
+        ws_raw = [tile("ws_raw%d" % s, [P, M], U8) for s in range(2)]
+        ws = [tile("ws%d" % s, [P, M], U8) for s in range(2)]
+        w2_raw = [tile("w2_raw%d" % a, [P, PACK, M // 2], F32) for a in range(2)]
+        w2_bf = [tile("w2_bf%d" % a, [P, PACK * M // 2], BF16) for a in range(2)]
+        w2_codes = tile("w2_codes", [P, M], U32)
+        w2_sc = tile("w2_sc", [P, M], U8)
+        bias = tile("bias", [P, PACK], F32)
+        keys = [(g, j) for g in range(GROUPS) for j in range(CHUNKS)]
+        x_raw = {k: tile("x_raw%d_%d" % k, [P, PACK, W], F32) for k in keys}
+        x_bf = {k: tile("x_bf%d_%d" % k, [P, PACK * W], BF16) for k in keys}
+        x_codes = {k: tile("x_codes%d_%d" % k, [P, W], U32) for k in keys}
+        x_sc = {k: tile("x_sc%d_%d" % k, [P, W], U8) for k in keys}
+        okeys = [(g, h) for g in range(GROUPS) for h in range(2)]
+        acc = {k: ps.tile([P, PACK * W], F32, name="acc%d_%d" % k) for k in okeys}
+        y = {k: tile("y%d_%d" % k, [P, PACK, W], F32) for k in okeys}
+        y_bf = {k: tile("y_bf%d_%d" % k, [P, PACK * W], BF16) for k in okeys}
+        y_codes = tile("y_codes", [P, T], U32)
+        y_sc = tile("y_sc", [P, T], U8)
+
+        x_rows = x.rearrange("(p j) t -> p j t", j=PACK)
+        w2_rows = w2.rearrange("(p j) n -> p j n", j=PACK)
+        out_rows = out_0.rearrange("(p r) t -> p r t", r=PACK)
+        out_words = out_1[0].rearrange("p t i -> p (t i)").bitcast(I32)
+
+        def load_x(g, j):
+            c0 = D * j + W * g
+            nc.sync.dma_start(out=x_raw[g, j][:], in_=x_rows[:, :, c0 : c0 + W])
+
+        def load_w2(a):
+            nc.sync.dma_start(out=w2_raw[a][:], in_=w2_rows[:, :, a * M // 2 : (a + 1) * M // 2])
+
+        def load_scales(dst, src):
+            for q in range(4):
+                nc.sync.dma_start(
+                    out=dst[32 * q : 32 * q + 4, :].bitcast(I32),
+                    in_=src[0, 4 * q : 4 * q + 4, :].bitcast(I32),
+                )
+
+        def cast(on_scalar, out, in_):
+            if on_scalar:
+                nc.scalar.activation(out=out, in_=in_, func=ACT.Copy)
+            else:
+                nc.vector.tensor_copy(out=out, in_=in_)
+
+        def interleave(on_scalar, dst, src):
+            cast(
+                on_scalar,
+                dst[:].rearrange("p (c i j) -> p c j i", i=4, j=PACK),
+                src[:].rearrange("p j (c i) -> p c j i", i=4),
+            )
+
+        def deal_w2(on_scalar, a):
+            cast(
+                on_scalar,
+                w2_bf[a][:].rearrange("p (r m j) -> p m r j", r=PACK, j=PACK),
+                w2_raw[a][:].rearrange("p j (m r) -> p m r j", r=PACK),
+            )
+
+        def quant_w2(a):
+            for r in range(PACK):
+                c0 = P * r + HALF_M * a
+                nc.vector.quantize_mx(
+                    out=w2_codes[:, c0 : c0 + HALF_M].bitcast(FP8X4),
+                    scales=w2_sc[:, c0 : c0 + HALF_M],
+                    in_=w2_bf[a][:, PACK * HALF_M * r : PACK * HALF_M * (r + 1)],
+                )
+
+        def quant_x(g, j):
+            nc.vector.quantize_mx(out=x_codes[g, j][:].bitcast(FP8X4), scales=x_sc[g, j][:], in_=x_bf[g, j][:])
+
+        def tap(g, h, s, first, final):
+            for r in range(PACK):
+                cols = slice(P * r, P * (r + 1))
+                if s == 0:
+                    lhsT = w0_codes[:, 2 * P * r : 2 * P * (r + 1)].bitcast(FP4X4)
+                    lhsT_scale = ws[0][:, cols]
+                elif s == 1:
+                    lhsT = w1_codes[:, cols].bitcast(FP8X4)
+                    lhsT_scale = ws[1][:, cols]
+                else:
+                    lhsT = w2_codes[:, cols].bitcast(FP8X4)
+                    lhsT_scale = w2_sc[:, cols]
+                nc.tensor.matmul_mx(
+                    out=acc[g, h][:, W * r : W * (r + 1)],
+                    lhsT=lhsT,
+                    lhsT_scale=lhsT_scale,
+                    rhs=x_codes[g, h + s][:].bitcast(FP8X4),
+                    rhs_scale=x_sc[g, h + s][:],
+                    start=(first and r == 0),
+                    stop=(final and r == PACK - 1),
+                )
+
+        def passes(g, j):
+            for h in range(2):
+                if 0 <= j - h <= 2:
+                    tap(g, h, j - h, j == ORDER[0], j in ORDER[2:])
+
+        def evacuate(g, h):
+            for r in range(PACK):
+                nc.scalar.activation(
+                    out=y[g, h][:, r, :],
+                    in_=acc[g, h][:, W * r : W * (r + 1)],
+                    func=ACT.Identity,
+                    bias=bias[:, r : r + 1],
+                )
+
+        def store_y(g, h):
+            c0 = D * h + W * g
+            nc.sync.dma_start(out=out_rows[:, :, c0 : c0 + W], in_=y[g, h][:])
+
+        def store_words(g0, g1):
+            nc.sync.dma_start(
+                out=out_words.rearrange("p (h t) -> p h t", h=2)[:, :, W * g0 : W * g1],
+                in_=y_codes[:].bitcast(I32).rearrange("p (h t) -> p h t", h=2)[:, :, W * g0 : W * g1],
+            )
+
+        def quant_y(g, h):
+            c0 = D * h + W * g
+            nc.vector.quantize_mx(
+                out=y_codes[:, c0 : c0 + W].bitcast(FP8X4), scales=y_sc[:, c0 : c0 + W], in_=y_bf[g, h][:]
+            )
+
+        def deal_scales(s):
+            nc.vector.tensor_copy(
+                out=ws[s][:].rearrange("p (r m) -> p r m", r=PACK),
+                in_=ws_raw[s][:].rearrange("p (m r) -> p r m", r=PACK),
+            )
+
+        def il(on_scalar, g, j):
+            interleave(on_scalar, x_bf[g, j], x_raw[g, j])
+
+        def qp(g, j):
+            quant_x(g, j)
+            passes(g, j)
+
+        def oil(on_scalar, g, h):
+            interleave(on_scalar, y_bf[g, h], y[g, h])
+
+        def warm_up(n):
+            for i in range(n):
+                nc.tensor.matmul_mx(
+                    out=acc[GROUPS - 1, 1][:],
+                    lhsT=w1_codes[:, 0:P].bitcast(FP8X4),
+                    lhsT_scale=ws[1][:, 0:P],
+                    rhs=w1_codes[:].bitcast(FP8X4),
+                    rhs_scale=ws[1][:],
+                    start=True,
+                    stop=True,
+                )
+
+        nc.vector.memset(ws_raw[1][:].bitcast(I32), 0)
+        nc.vector.memset(ws_raw[0][:].bitcast(I32), 0)
+        nc.gpsimd.dma_start(out=bias[:], in_=b.rearrange("(p r) -> p r", r=PACK))
+        nc.sync.dma_start(out=w1_raw[:].bitcast(I32), in_=w1_words[0].rearrange("p n i -> p (n i)").bitcast(I32))
+        load_scales(ws_raw[1], w1_scales)
+        load_w2(0)
+        nc.sync.dma_start(out=w0_raw[:].bitcast(I32), in_=w0_words[0].bitcast(I32))
+        seq = [(g, j) for g in range(GROUPS) for j in ORDER]
+        load_x(*seq[0])
+        load_scales(ws_raw[0], w0_scales)
+        load_w2(1)
+        for k in seq[1:]:
+            load_x(*k)
+
+        nc.vector.tensor_copy(
+            out=w1_codes[:].bitcast(I32).rearrange("p (r a i) -> p a r i", r=PACK, i=4),
+            in_=w1_raw[:].bitcast(I32).rearrange("p (a i r) -> p a r i", r=PACK, i=4),
+        )
+        deal_scales(1)
+        warm_up(6)
+        deal_w2(True, 0)
+        nc.vector.tensor_copy(
+            out=w0_codes[:].rearrange("p (r m e) -> p r m e", r=PACK, e=2),
+            in_=w0_raw[:].rearrange("p (m r e) -> p r m e", r=PACK, e=2),
+        )
+        il(False, *seq[0])
+        deal_scales(0)
+        qp(*seq[0])
+        quant_w2(0)
+        deal_w2(False, 1)
+        il(True, *seq[1])
+        quant_w2(1)
+        il(True, *seq[2])
+        qp(*seq[1])
+        il(False, *seq[3])
+        qp(*seq[2])
+        for g in range(1, GROUPS):
+            n = 4 * g
+            last = g == GROUPS - 1
+            il(False, *seq[n])
+            qp(*seq[n - 1])
+            evacuate(g - 1, 0)
+            store_y(g - 1, 0)
+            evacuate(g - 1, 1)
+            store_y(g - 1, 1)
+            oil(True, g - 1, 0)
+            il(False, *seq[n + 1])
+            qp(*seq[n])
+            il(False, *seq[n + 2])
+            qp(*seq[n + 1])
+            if last:
+                qp(*seq[n + 2])
+                il(False, *seq[n + 3])
+                quant_y(0, 0)
+                qp(*seq[n + 3])
+            else:
+                il(False, *seq[n + 3])
+                qp(*seq[n + 2])
+
+        g = GROUPS - 1
+        oil(False, 0, 1)
+        quant_y(1, 0)
+        oil(False, 1, 1)
+        quant_y(0, 1)
+        oil(False, 2, 1)
+        quant_y(1, 1)
+        store_words(0, 2)
+        evacuate(g, 0)
+        store_y(g, 0)
+        evacuate(g, 1)
+        store_y(g, 1)
+        quant_y(2, 0)
+        oil(False, g, 0)
+        quant_y(2, 1)
+        quant_y(g, 0)
+        oil(False, g, 1)
+        quant_y(g, 1)
+        store_words(2, 4)
+        for q in range(4):
+            eng = nc.sync if q % 2 == 0 else nc.scalar
+            eng.dma_start(
+                out=out_2[0, 4 * q : 4 * q + 4, :].bitcast(I32),
+                in_=y_sc[32 * q : 32 * q + 4, :].bitcast(I32),
+            )

@@ -21,6 +21,8 @@ GROUPS = D // W
 CHUNKS = 4
 HALF_M = P // 2
 ORDER = (1, 2, 0, 3)
+LOADS = [(1,0,2),(2,0,2),(0,0,2),(3,0,2),(1,2,2),(2,2,2),(0,2,2),(3,2,2)]
+STORES = [(0,0,2),(1,0,2),(0,2,2),(1,2,2)]
 
 
 def tile_mix_dconv_fm_pl_bias_kernel(
@@ -41,19 +43,21 @@ def tile_mix_dconv_fm_pl_bias_kernel(
         w1_codes = tile("w1_codes", [P, M], U32)
         ws_raw = [tile("ws_raw%d" % s, [P, M], U8) for s in range(2)]
         ws = [tile("ws%d" % s, [P, M], U8) for s in range(2)]
-        w2_raw = [tile("w2_raw%d" % a, [P, PACK, M // 2], F32) for a in range(2)]
+        w2_raw = tile("w2_raw", [P, PACK, M], F32)
         w2_bf = [tile("w2_bf%d" % a, [P, PACK * M // 2], BF16) for a in range(2)]
         w2_codes = tile("w2_codes", [P, M], U32)
         w2_sc = tile("w2_sc", [P, M], U8)
         bias = tile("bias", [P, PACK], F32)
         keys = [(g, j) for g in range(GROUPS) for j in range(CHUNKS)]
-        x_raw = {k: tile("x_raw%d_%d" % k, [P, PACK, W], F32) for k in keys}
+        x_raw = {(j, g0): tile("x_raw%d_%d" % (j, g0), [P, PACK, W * n], F32) for j, g0, n in LOADS}
+        x_view = {(g0 + i, j): x_raw[j, g0][:, :, W * i : W * (i + 1)] for j, g0, n in LOADS for i in range(n)}
         x_bf = {k: tile("x_bf%d_%d" % k, [P, PACK * W], BF16) for k in keys}
         x_codes = {k: tile("x_codes%d_%d" % k, [P, W], U32) for k in keys}
         x_sc = {k: tile("x_sc%d_%d" % k, [P, W], U8) for k in keys}
         okeys = [(g, h) for g in range(GROUPS) for h in range(2)]
         acc = {k: ps.tile([P, PACK * W], F32, name="acc%d_%d" % k) for k in okeys}
-        y = {k: tile("y%d_%d" % k, [P, PACK, W], F32) for k in okeys}
+        y_tile = {(h, g0): tile("y%d_%d" % (h, g0), [P, PACK, W * n], F32) for h, g0, n in STORES}
+        y = {(g0 + i, h): y_tile[h, g0][:, :, W * i : W * (i + 1)] for h, g0, n in STORES for i in range(n)}
         y_bf = {k: tile("y_bf%d_%d" % k, [P, PACK * W], BF16) for k in okeys}
         y_codes = tile("y_codes", [P, T], U32)
         y_sc = tile("y_sc", [P, T], U8)
@@ -63,12 +67,10 @@ def tile_mix_dconv_fm_pl_bias_kernel(
         out_rows = out_0.rearrange("(p r) t -> p r t", r=PACK)
         out_words = out_1[0].rearrange("p t i -> p (t i)").bitcast(I32)
 
-        def load_x(g, j):
-            c0 = D * j + W * g
-            nc.sync.dma_start(out=x_raw[g, j][:], in_=x_rows[:, :, c0 : c0 + W])
+        def load_x(j, g0, n):
+            c0 = D * j + W * g0
+            nc.sync.dma_start(out=x_raw[j, g0][:], in_=x_rows[:, :, c0 : c0 + W * n])
 
-        def load_w2(a):
-            nc.sync.dma_start(out=w2_raw[a][:], in_=w2_rows[:, :, a * M // 2 : (a + 1) * M // 2])
 
         def load_scales(dst, src):
             for q in range(4):
@@ -87,14 +89,14 @@ def tile_mix_dconv_fm_pl_bias_kernel(
             cast(
                 on_scalar,
                 dst[:].rearrange("p (c i j) -> p c j i", i=4, j=PACK),
-                src[:].rearrange("p j (c i) -> p c j i", i=4),
+                src.rearrange("p j (c i) -> p c j i", i=4),
             )
 
         def deal_w2(on_scalar, a):
             cast(
                 on_scalar,
                 w2_bf[a][:].rearrange("p (r m j) -> p m r j", r=PACK, j=PACK),
-                w2_raw[a][:].rearrange("p j (m r) -> p m r j", r=PACK),
+                w2_raw[:, :, a * M // 2 : (a + 1) * M // 2].rearrange("p j (m r) -> p m r j", r=PACK),
             )
 
         def quant_w2(a):
@@ -131,23 +133,28 @@ def tile_mix_dconv_fm_pl_bias_kernel(
                     stop=(final and r == PACK - 1),
                 )
 
-        def passes(g, j):
-            for h in range(2):
-                if 0 <= j - h <= 2:
-                    tap(g, h, j - h, j == ORDER[0], j in ORDER[2:])
-
-        def evacuate(g, h):
-            for r in range(PACK):
-                nc.scalar.activation(
-                    out=y[g, h][:, r, :],
-                    in_=acc[g, h][:, W * r : W * (r + 1)],
-                    func=ACT.Identity,
-                    bias=bias[:, r : r + 1],
+        def evacuate(on_scalar, g, h):
+            if on_scalar:
+                for r in range(PACK):
+                    nc.scalar.activation(
+                        out=y[g, h][:, r, :],
+                        in_=acc[g, h][:, W * r : W * (r + 1)],
+                        func=ACT.Identity,
+                        bias=bias[:, r : r + 1],
+                    )
+            else:
+                nc.vector.tensor_tensor(
+                    out=y[g, h],
+                    in0=acc[g, h][:].rearrange("p (r c) -> p r c", r=PACK),
+                    in1=bias[:].unsqueeze(2).to_broadcast([P, PACK, W]),
+                    op=mybir.AluOpType.add,
                 )
 
         def store_y(g, h):
-            c0 = D * h + W * g
-            nc.sync.dma_start(out=out_rows[:, :, c0 : c0 + W], in_=y[g, h][:])
+            for hh, g0, n in STORES:
+                if hh == h and g0 + n - 1 == g:
+                    c0 = D * h + W * g0
+                    nc.sync.dma_start(out=out_rows[:, :, c0 : c0 + W * n], in_=y_tile[h, g0][:])
 
         def store_words(g0, g1):
             nc.sync.dma_start(
@@ -168,104 +175,129 @@ def tile_mix_dconv_fm_pl_bias_kernel(
             )
 
         def il(on_scalar, g, j):
-            interleave(on_scalar, x_bf[g, j], x_raw[g, j])
-
-        def qp(g, j):
-            quant_x(g, j)
-            passes(g, j)
+            interleave(on_scalar, x_bf[g, j], x_view[g, j])
 
         def oil(on_scalar, g, h):
             interleave(on_scalar, y_bf[g, h], y[g, h])
 
-        def warm_up(n):
-            for i in range(n):
-                nc.tensor.matmul_mx(
-                    out=acc[GROUPS - 1, 1][:],
-                    lhsT=w1_codes[:, 0:P].bitcast(FP8X4),
-                    lhsT_scale=ws[1][:, 0:P],
-                    rhs=w1_codes[:].bitcast(FP8X4),
-                    rhs_scale=ws[1][:],
-                    start=True,
-                    stop=True,
-                )
+        def deal_w1():
+            nc.vector.tensor_copy(
+                out=w1_codes[:].bitcast(I32).rearrange("p (r a i) -> p a r i", r=PACK, i=4),
+                in_=w1_raw[:].bitcast(I32).rearrange("p (a i r) -> p a r i", r=PACK, i=4),
+            )
+
+        def deal_w0():
+            nc.vector.tensor_copy(
+                out=w0_codes[:].rearrange("p (r m e) -> p r m e", r=PACK, e=2),
+                in_=w0_raw[:].rearrange("p (m r e) -> p r m e", r=PACK, e=2),
+            )
 
         nc.vector.memset(ws_raw[1][:].bitcast(I32), 0)
         nc.vector.memset(ws_raw[0][:].bitcast(I32), 0)
-        nc.gpsimd.dma_start(out=bias[:], in_=b.rearrange("(p r) -> p r", r=PACK))
-        nc.sync.dma_start(out=w1_raw[:].bitcast(I32), in_=w1_words[0].rearrange("p n i -> p (n i)").bitcast(I32))
+        load_x(*LOADS[0])
         load_scales(ws_raw[1], w1_scales)
-        load_w2(0)
+        nc.sync.dma_start(out=w1_raw[:].bitcast(I32), in_=w1_words[0].rearrange("p n i -> p (n i)").bitcast(I32))
         nc.sync.dma_start(out=w0_raw[:].bitcast(I32), in_=w0_words[0].bitcast(I32))
-        seq = [(g, j) for g in range(GROUPS) for j in ORDER]
-        load_x(*seq[0])
+        nc.sync.dma_start(out=w2_raw[:], in_=w2_rows)
         load_scales(ws_raw[0], w0_scales)
-        load_w2(1)
-        for k in seq[1:]:
+        load_x(*LOADS[1])
+        nc.sync.dma_start(out=bias[:], in_=b.rearrange("(p r) -> p r", r=PACK))
+        for k in LOADS[2:]:
             load_x(*k)
 
-        nc.vector.tensor_copy(
-            out=w1_codes[:].bitcast(I32).rearrange("p (r a i) -> p a r i", r=PACK, i=4),
-            in_=w1_raw[:].bitcast(I32).rearrange("p (a i r) -> p a r i", r=PACK, i=4),
-        )
+        il(False, 0, 1)
+        il(True, 1, 1)
         deal_scales(1)
-        warm_up(6)
+        deal_w1()
+        quant_x(0, 1)
+        quant_x(1, 1)
+        tap(0, 0, 1, True, False)
+        tap(1, 0, 1, True, False)
+        deal_w0()
         deal_w2(True, 0)
-        nc.vector.tensor_copy(
-            out=w0_codes[:].rearrange("p (r m e) -> p r m e", r=PACK, e=2),
-            in_=w0_raw[:].rearrange("p (m r e) -> p r m e", r=PACK, e=2),
-        )
-        il(False, *seq[0])
-        deal_scales(0)
-        qp(*seq[0])
-        quant_w2(0)
         deal_w2(False, 1)
-        il(True, *seq[1])
+        deal_scales(0)
+        tap(0, 1, 0, True, False)
+        tap(1, 1, 0, True, False)
         quant_w2(1)
-        il(True, *seq[2])
-        qp(*seq[1])
-        il(False, *seq[3])
-        qp(*seq[2])
-        for g in range(1, GROUPS):
-            n = 4 * g
-            last = g == GROUPS - 1
-            il(False, *seq[n])
-            qp(*seq[n - 1])
-            evacuate(g - 1, 0)
-            store_y(g - 1, 0)
-            evacuate(g - 1, 1)
-            store_y(g - 1, 1)
-            oil(True, g - 1, 0)
-            il(False, *seq[n + 1])
-            qp(*seq[n])
-            il(False, *seq[n + 2])
-            qp(*seq[n + 1])
-            if last:
-                qp(*seq[n + 2])
-                il(False, *seq[n + 3])
-                quant_y(0, 0)
-                qp(*seq[n + 3])
-            else:
-                il(False, *seq[n + 3])
-                qp(*seq[n + 2])
-
-        g = GROUPS - 1
-        oil(False, 0, 1)
+        il(False, 0, 2)
+        il(True, 1, 2)
+        quant_w2(0)
+        quant_x(0, 2)
+        quant_x(1, 2)
+        tap(0, 0, 2, False, False)
+        tap(1, 0, 2, False, False)
+        tap(0, 1, 1, False, False)
+        il(False, 0, 0)
+        il(True, 1, 0)
+        quant_x(0, 0)
+        tap(0, 0, 0, False, True)
+        tap(1, 1, 1, False, False)
+        quant_x(1, 0)
+        tap(1, 0, 0, False, True)
+        il(False, 0, 3)
+        il(False, 1, 3)
+        quant_x(0, 3)
+        tap(0, 1, 2, False, True)
+        quant_x(1, 3)
+        tap(1, 1, 2, False, True)
+        evacuate(True, 0, 0)
+        evacuate(True, 1, 0)
+        store_y(1, 0)
+        evacuate(True, 0, 1)
+        evacuate(True, 1, 1)
+        store_y(1, 1)
+        il(False, 2, 1)
+        il(False, 3, 1)
+        quant_x(2, 1)
+        tap(2, 0, 1, True, False)
+        tap(2, 1, 0, True, False)
+        quant_x(3, 1)
+        tap(3, 0, 1, True, False)
+        tap(3, 1, 0, True, False)
+        oil(False, 0, 0)
+        il(False, 2, 2)
+        il(False, 3, 2)
+        quant_x(2, 2)
+        tap(2, 0, 2, False, False)
+        quant_x(3, 2)
+        tap(3, 0, 2, False, False)
+        tap(2, 1, 1, False, False)
+        tap(3, 1, 1, False, False)
+        oil(True, 1, 0)
+        oil(True, 0, 1)
+        quant_y(0, 0)
+        il(False, 2, 0)
+        il(False, 3, 0)
+        quant_x(2, 0)
+        tap(2, 0, 0, False, True)
+        quant_x(3, 0)
+        tap(3, 0, 0, False, True)
         quant_y(1, 0)
+        il(False, 2, 3)
+        il(True, 3, 3)
         oil(False, 1, 1)
+        quant_x(2, 3)
+        tap(2, 1, 2, False, True)
         quant_y(0, 1)
-        oil(False, 2, 1)
+        quant_x(3, 3)
+        tap(3, 1, 2, False, True)
         quant_y(1, 1)
         store_words(0, 2)
-        evacuate(g, 0)
-        store_y(g, 0)
-        evacuate(g, 1)
-        store_y(g, 1)
+        evacuate(True, 2, 0)
+        evacuate(False, 3, 0)
+        store_y(3, 0)
+        evacuate(True, 2, 1)
+        oil(False, 2, 0)
+        evacuate(True, 3, 1)
+        store_y(3, 1)
+        oil(False, 3, 0)
         quant_y(2, 0)
-        oil(False, g, 0)
+        oil(False, 2, 1)
+        quant_y(3, 0)
+        oil(False, 3, 1)
         quant_y(2, 1)
-        quant_y(g, 0)
-        oil(False, g, 1)
-        quant_y(g, 1)
+        quant_y(3, 1)
         store_words(2, 4)
         for q in range(4):
             eng = nc.sync if q % 2 == 0 else nc.scalar

@@ -16,13 +16,15 @@ ACT = mybir.ActivationFunctionType
 
 P = 128
 PACK = 4
-W = 128
-GROUPS = D // W
-CHUNKS = 4
-HALF_M = P // 2
-ORDER = (1, 2, 0, 3)
-LOADS = [(1,0,2),(2,0,2),(0,0,2),(3,0,2),(1,2,2),(2,2,2),(0,2,2),(3,2,2)]
-STORES = [(0,0,2),(1,0,2),(0,2,2),(1,2,2)]
+LINE = 4
+QUADRANTS = 4
+TAPS = 3
+BLOCK = 128
+SLAB = 2 * BLOCK
+SLABS = D // SLAB
+HALVES = T // D
+W2_PART = P // 2
+WINDOW_ORDER = (1, 2, 0, 3)
 
 
 def tile_mix_dconv_fm_pl_bias_kernel(
@@ -37,153 +39,65 @@ def tile_mix_dconv_fm_pl_bias_kernel(
         def tile(name, shape, dtype):
             return sb.tile(shape, dtype, name=name, align_bytes=64)
 
+        def blocks(slab):
+            return (2 * slab, 2 * slab + 1)
+
+        def within_slab(slab_tile, g):
+            c0 = BLOCK * (g % 2)
+            return slab_tile[:, :, c0 : c0 + BLOCK]
+
         w0_raw = tile("w0_raw", [P, 2 * M], U8)
         w0_codes = tile("w0_codes", [P, 2 * M], U8)
         w1_raw = tile("w1_raw", [P, M], U32)
         w1_codes = tile("w1_codes", [P, M], U32)
-        ws_raw = [tile("ws_raw%d" % s, [P, M], U8) for s in range(2)]
-        ws = [tile("ws%d" % s, [P, M], U8) for s in range(2)]
+        packed_sc_raw = [tile("packed_sc_raw%d" % s, [P, M], U8) for s in range(2)]
+        packed_sc = [tile("packed_sc%d" % s, [P, M], U8) for s in range(2)]
         w2_raw = tile("w2_raw", [P, PACK, M], F32)
-        w2_bf = [tile("w2_bf%d" % a, [P, PACK * M // 2], BF16) for a in range(2)]
+        w2_bf = [tile("w2_bf%d" % part, [P, PACK * W2_PART * PACK], BF16) for part in range(2)]
         w2_codes = tile("w2_codes", [P, M], U32)
         w2_sc = tile("w2_sc", [P, M], U8)
         bias = tile("bias", [P, PACK], F32)
-        keys = [(g, j) for g in range(GROUPS) for j in range(CHUNKS)]
-        x_raw = {(j, g0): tile("x_raw%d_%d" % (j, g0), [P, PACK, W * n], F32) for j, g0, n in LOADS}
-        x_view = {(g0 + i, j): x_raw[j, g0][:, :, W * i : W * (i + 1)] for j, g0, n in LOADS for i in range(n)}
-        x_bf = {k: tile("x_bf%d_%d" % k, [P, PACK * W], BF16) for k in keys}
-        x_codes = {k: tile("x_codes%d_%d" % k, [P, W], U32) for k in keys}
-        x_sc = {k: tile("x_sc%d_%d" % k, [P, W], U8) for k in keys}
-        okeys = [(g, h) for g in range(GROUPS) for h in range(2)]
-        acc = {k: ps.tile([P, PACK * W], F32, name="acc%d_%d" % k) for k in okeys}
-        y_tile = {(h, g0): tile("y%d_%d" % (h, g0), [P, PACK, W * n], F32) for h, g0, n in STORES}
-        y = {(g0 + i, h): y_tile[h, g0][:, :, W * i : W * (i + 1)] for h, g0, n in STORES for i in range(n)}
-        y_bf = {k: tile("y_bf%d_%d" % k, [P, PACK * W], BF16) for k in okeys}
+
+        x_loads = [(slab, j) for slab in range(SLABS) for j in WINDOW_ORDER]
+        x_raw = {key: tile("x_raw%d_%d" % key, [P, PACK, SLAB], F32) for key in x_loads}
+        x_keys = [(g, j) for slab, j in x_loads for g in blocks(slab)]
+        x_bf = {key: tile("x_bf%d_%d" % key, [P, PACK * BLOCK], BF16) for key in x_keys}
+        x_codes = {key: tile("x_codes%d_%d" % key, [P, BLOCK], U32) for key in x_keys}
+        x_sc = {key: tile("x_sc%d_%d" % key, [P, BLOCK], U8) for key in x_keys}
+
+        y_keys = [(g, h) for g in range(2 * SLABS) for h in range(HALVES)]
+        acc = {key: ps.tile([P, PACK * BLOCK], F32, name="acc%d_%d" % key) for key in y_keys}
+        y = {(slab, h): tile("y%d_%d" % (slab, h), [P, PACK, SLAB], F32) for slab in range(SLABS) for h in range(HALVES)}
+        y_bf = {key: tile("y_bf%d_%d" % key, [P, PACK * BLOCK], BF16) for key in y_keys}
         y_codes = tile("y_codes", [P, T], U32)
         y_sc = tile("y_sc", [P, T], U8)
 
-        x_rows = x.rearrange("(p j) t -> p j t", j=PACK)
-        w2_rows = w2.rearrange("(p j) n -> p j n", j=PACK)
+        x_rows = x.rearrange("(p i) t -> p i t", i=PACK)
         out_rows = out_0.rearrange("(p r) t -> p r t", r=PACK)
         out_words = out_1[0].rearrange("p t i -> p (t i)").bitcast(I32)
 
-        def load_x(j, g0, n):
-            c0 = D * j + W * g0
-            nc.sync.dma_start(out=x_raw[j, g0][:], in_=x_rows[:, :, c0 : c0 + W * n])
+        def load_x(slab, j):
+            c0 = D * j + SLAB * slab
+            nc.sync.dma_start(out=x_raw[slab, j][:], in_=x_rows[:, :, c0 : c0 + SLAB])
 
-
-        def load_scales(dst, src):
-            for q in range(4):
+        def load_scales(s, src):
+            for q in range(QUADRANTS):
                 nc.sync.dma_start(
-                    out=dst[32 * q : 32 * q + 4, :].bitcast(I32),
+                    out=packed_sc_raw[s][32 * q : 32 * q + 4, :].bitcast(I32),
                     in_=src[0, 4 * q : 4 * q + 4, :].bitcast(I32),
                 )
 
-        def cast(on_scalar, out, in_):
+        def round_to_bf16(on_scalar, out, in_):
             if on_scalar:
                 nc.scalar.activation(out=out, in_=in_, func=ACT.Copy)
             else:
                 nc.vector.tensor_copy(out=out, in_=in_)
 
         def interleave(on_scalar, dst, src):
-            cast(
+            round_to_bf16(
                 on_scalar,
-                dst[:].rearrange("p (c i j) -> p c j i", i=4, j=PACK),
-                src.rearrange("p j (c i) -> p c j i", i=4),
-            )
-
-        def deal_w2(on_scalar, a):
-            cast(
-                on_scalar,
-                w2_bf[a][:].rearrange("p (r m j) -> p m r j", r=PACK, j=PACK),
-                w2_raw[:, :, a * M // 2 : (a + 1) * M // 2].rearrange("p j (m r) -> p m r j", r=PACK),
-            )
-
-        def quant_w2(a):
-            for r in range(PACK):
-                c0 = P * r + HALF_M * a
-                nc.vector.quantize_mx(
-                    out=w2_codes[:, c0 : c0 + HALF_M].bitcast(FP8X4),
-                    scales=w2_sc[:, c0 : c0 + HALF_M],
-                    in_=w2_bf[a][:, PACK * HALF_M * r : PACK * HALF_M * (r + 1)],
-                )
-
-        def quant_x(g, j):
-            nc.vector.quantize_mx(out=x_codes[g, j][:].bitcast(FP8X4), scales=x_sc[g, j][:], in_=x_bf[g, j][:])
-
-        def tap(g, h, s, first, final):
-            for r in range(PACK):
-                cols = slice(P * r, P * (r + 1))
-                if s == 0:
-                    lhsT = w0_codes[:, 2 * P * r : 2 * P * (r + 1)].bitcast(FP4X4)
-                    lhsT_scale = ws[0][:, cols]
-                elif s == 1:
-                    lhsT = w1_codes[:, cols].bitcast(FP8X4)
-                    lhsT_scale = ws[1][:, cols]
-                else:
-                    lhsT = w2_codes[:, cols].bitcast(FP8X4)
-                    lhsT_scale = w2_sc[:, cols]
-                nc.tensor.matmul_mx(
-                    out=acc[g, h][:, W * r : W * (r + 1)],
-                    lhsT=lhsT,
-                    lhsT_scale=lhsT_scale,
-                    rhs=x_codes[g, h + s][:].bitcast(FP8X4),
-                    rhs_scale=x_sc[g, h + s][:],
-                    start=(first and r == 0),
-                    stop=(final and r == PACK - 1),
-                )
-
-        def evacuate(on_scalar, g, h):
-            if on_scalar:
-                for r in range(PACK):
-                    nc.scalar.activation(
-                        out=y[g, h][:, r, :],
-                        in_=acc[g, h][:, W * r : W * (r + 1)],
-                        func=ACT.Identity,
-                        bias=bias[:, r : r + 1],
-                    )
-            else:
-                nc.vector.tensor_tensor(
-                    out=y[g, h],
-                    in0=acc[g, h][:].rearrange("p (r c) -> p r c", r=PACK),
-                    in1=bias[:].unsqueeze(2).to_broadcast([P, PACK, W]),
-                    op=mybir.AluOpType.add,
-                )
-
-        def store_y(g, h):
-            for hh, g0, n in STORES:
-                if hh == h and g0 + n - 1 == g:
-                    c0 = D * h + W * g0
-                    nc.sync.dma_start(out=out_rows[:, :, c0 : c0 + W * n], in_=y_tile[h, g0][:])
-
-        def store_words(g0, g1):
-            nc.sync.dma_start(
-                out=out_words.rearrange("p (h t) -> p h t", h=2)[:, :, W * g0 : W * g1],
-                in_=y_codes[:].bitcast(I32).rearrange("p (h t) -> p h t", h=2)[:, :, W * g0 : W * g1],
-            )
-
-        def quant_y(g, h):
-            c0 = D * h + W * g
-            nc.vector.quantize_mx(
-                out=y_codes[:, c0 : c0 + W].bitcast(FP8X4), scales=y_sc[:, c0 : c0 + W], in_=y_bf[g, h][:]
-            )
-
-        def deal_scales(s):
-            nc.vector.tensor_copy(
-                out=ws[s][:].rearrange("p (r m) -> p r m", r=PACK),
-                in_=ws_raw[s][:].rearrange("p (m r) -> p r m", r=PACK),
-            )
-
-        def il(on_scalar, g, j):
-            interleave(on_scalar, x_bf[g, j], x_view[g, j])
-
-        def oil(on_scalar, g, h):
-            interleave(on_scalar, y_bf[g, h], y[g, h])
-
-        def deal_w1():
-            nc.vector.tensor_copy(
-                out=w1_codes[:].bitcast(I32).rearrange("p (r a i) -> p a r i", r=PACK, i=4),
-                in_=w1_raw[:].bitcast(I32).rearrange("p (a i r) -> p a r i", r=PACK, i=4),
+                dst[:].rearrange("p (c e i) -> p c i e", e=LINE, i=PACK),
+                src.rearrange("p i (c e) -> p c i e", e=LINE),
             )
 
         def deal_w0():
@@ -192,116 +106,187 @@ def tile_mix_dconv_fm_pl_bias_kernel(
                 in_=w0_raw[:].rearrange("p (m r e) -> p r m e", r=PACK, e=2),
             )
 
-        nc.vector.memset(ws_raw[1][:].bitcast(I32), 0)
-        nc.vector.memset(ws_raw[0][:].bitcast(I32), 0)
-        load_x(*LOADS[0])
-        load_scales(ws_raw[1], w1_scales)
+        def deal_w1():
+            nc.vector.tensor_copy(
+                out=w1_codes[:].bitcast(I32).rearrange("p (r a e) -> p a r e", r=PACK, e=LINE),
+                in_=w1_raw[:].bitcast(I32).rearrange("p (a e r) -> p a r e", r=PACK, e=LINE),
+            )
+
+        def deal_scales(s):
+            nc.vector.tensor_copy(
+                out=packed_sc[s][:].rearrange("p (r m) -> p r m", r=PACK),
+                in_=packed_sc_raw[s][:].rearrange("p (m r) -> p r m", r=PACK),
+            )
+
+        def round_w2(on_scalar, part):
+            round_to_bf16(
+                on_scalar,
+                w2_bf[part][:].rearrange("p (r m i) -> p m r i", r=PACK, i=PACK),
+                w2_raw[:, :, part * M // 2 : (part + 1) * M // 2].rearrange("p i (m r) -> p m r i", r=PACK),
+            )
+
+        def quantize_w2(part):
+            for r in range(PACK):
+                c0 = P * r + W2_PART * part
+                nc.vector.quantize_mx(
+                    out=w2_codes[:, c0 : c0 + W2_PART].bitcast(FP8X4),
+                    scales=w2_sc[:, c0 : c0 + W2_PART],
+                    in_=w2_bf[part][:, PACK * W2_PART * r : PACK * W2_PART * (r + 1)],
+                )
+
+        def round_x(slab, j, share_with_scalar):
+            first, second = blocks(slab)
+            interleave(False, x_bf[first, j], within_slab(x_raw[slab, j], first))
+            interleave(share_with_scalar, x_bf[second, j], within_slab(x_raw[slab, j], second))
+
+        def quantize_x(g, j):
+            nc.vector.quantize_mx(out=x_codes[g, j][:].bitcast(FP8X4), scales=x_sc[g, j][:], in_=x_bf[g, j][:])
+
+        def product(g, h, s):
+            j = h + s
+            for r in range(PACK):
+                cols = slice(P * r, P * (r + 1))
+                if s == 0:
+                    lhsT = w0_codes[:, 2 * P * r : 2 * P * (r + 1)].bitcast(FP4X4)
+                    lhsT_scale = packed_sc[0][:, cols]
+                elif s == 1:
+                    lhsT = w1_codes[:, cols].bitcast(FP8X4)
+                    lhsT_scale = packed_sc[1][:, cols]
+                else:
+                    lhsT = w2_codes[:, cols].bitcast(FP8X4)
+                    lhsT_scale = w2_sc[:, cols]
+                nc.tensor.matmul_mx(
+                    out=acc[g, h][:, BLOCK * r : BLOCK * (r + 1)],
+                    lhsT=lhsT,
+                    lhsT_scale=lhsT_scale,
+                    rhs=x_codes[g, j][:].bitcast(FP8X4),
+                    rhs_scale=x_sc[g, j][:],
+                    start=(j == WINDOW_ORDER[0] and r == 0),
+                    stop=(j == TAPS * h and r == PACK - 1),
+                )
+
+        def products(slab, h, s):
+            for g in blocks(slab):
+                product(g, h, s)
+
+        def quantize_and_multiply(slab, h, s):
+            for g in blocks(slab):
+                quantize_x(g, h + s)
+                product(g, h, s)
+
+        def empty_bank(on_scalar, g, h):
+            dst = within_slab(y[g // 2, h], g)
+            if on_scalar:
+                for r in range(PACK):
+                    nc.scalar.activation(
+                        out=dst[:, r, :],
+                        in_=acc[g, h][:, BLOCK * r : BLOCK * (r + 1)],
+                        func=ACT.Identity,
+                        bias=bias[:, r : r + 1],
+                    )
+            else:
+                nc.vector.tensor_tensor(
+                    out=dst,
+                    in0=acc[g, h][:].rearrange("p (r c) -> p r c", r=PACK),
+                    in1=bias[:].unsqueeze(2).to_broadcast([P, PACK, BLOCK]),
+                    op=mybir.AluOpType.add,
+                )
+
+        def round_y(on_scalar, g, h):
+            interleave(on_scalar, y_bf[g, h], within_slab(y[g // 2, h], g))
+
+        def quantize_y(g, h):
+            c0 = D * h + BLOCK * g
+            nc.vector.quantize_mx(
+                out=y_codes[:, c0 : c0 + BLOCK].bitcast(FP8X4), scales=y_sc[:, c0 : c0 + BLOCK], in_=y_bf[g, h][:]
+            )
+
+        def store_y(slab, h):
+            c0 = D * h + SLAB * slab
+            nc.sync.dma_start(out=out_rows[:, :, c0 : c0 + SLAB], in_=y[slab, h][:])
+
+        def store_words(slab):
+            cols = slice(SLAB * slab, SLAB * (slab + 1))
+            nc.sync.dma_start(
+                out=out_words.rearrange("p (h t) -> p h t", h=HALVES)[:, :, cols],
+                in_=y_codes[:].bitcast(I32).rearrange("p (h t) -> p h t", h=HALVES)[:, :, cols],
+            )
+
+        nc.vector.memset(packed_sc_raw[1][:].bitcast(I32), 0)
+        nc.vector.memset(packed_sc_raw[0][:].bitcast(I32), 0)
+        load_x(*x_loads[0])
+        load_scales(1, w1_scales)
         nc.sync.dma_start(out=w1_raw[:].bitcast(I32), in_=w1_words[0].rearrange("p n i -> p (n i)").bitcast(I32))
         nc.sync.dma_start(out=w0_raw[:].bitcast(I32), in_=w0_words[0].bitcast(I32))
-        nc.sync.dma_start(out=w2_raw[:], in_=w2_rows)
-        load_scales(ws_raw[0], w0_scales)
-        load_x(*LOADS[1])
+        nc.sync.dma_start(out=w2_raw[:], in_=w2.rearrange("(p i) n -> p i n", i=PACK))
+        load_scales(0, w0_scales)
+        load_x(*x_loads[1])
         nc.sync.dma_start(out=bias[:], in_=b.rearrange("(p r) -> p r", r=PACK))
-        for k in LOADS[2:]:
-            load_x(*k)
+        for key in x_loads[2:]:
+            load_x(*key)
 
-        il(False, 0, 1)
-        il(True, 1, 1)
+        round_x(0, 1, share_with_scalar=True)
         deal_scales(1)
         deal_w1()
-        quant_x(0, 1)
-        quant_x(1, 1)
-        tap(0, 0, 1, True, False)
-        tap(1, 0, 1, True, False)
+        quantize_and_multiply(0, 0, 1)
         deal_w0()
-        deal_w2(True, 0)
-        deal_w2(False, 1)
+        round_w2(True, 0)
+        round_w2(False, 1)
         deal_scales(0)
-        tap(0, 1, 0, True, False)
-        tap(1, 1, 0, True, False)
-        quant_w2(1)
-        il(False, 0, 2)
-        il(True, 1, 2)
-        quant_w2(0)
-        quant_x(0, 2)
-        quant_x(1, 2)
-        tap(0, 0, 2, False, False)
-        tap(1, 0, 2, False, False)
-        tap(0, 1, 1, False, False)
-        il(False, 0, 0)
-        il(True, 1, 0)
-        quant_x(0, 0)
-        tap(0, 0, 0, False, True)
-        tap(1, 1, 1, False, False)
-        quant_x(1, 0)
-        tap(1, 0, 0, False, True)
-        il(False, 0, 3)
-        il(False, 1, 3)
-        quant_x(0, 3)
-        tap(0, 1, 2, False, True)
-        quant_x(1, 3)
-        tap(1, 1, 2, False, True)
-        evacuate(True, 0, 0)
-        evacuate(True, 1, 0)
+        products(0, 1, 0)
+        quantize_w2(1)
+        round_x(0, 2, share_with_scalar=True)
+        quantize_w2(0)
+        quantize_and_multiply(0, 0, 2)
+        round_x(0, 0, share_with_scalar=True)
+        quantize_and_multiply(0, 0, 0)
+        products(0, 1, 1)
+        round_x(0, 3, share_with_scalar=False)
+        quantize_and_multiply(0, 1, 2)
+        for h in range(HALVES):
+            for g in blocks(0):
+                empty_bank(True, g, h)
+            store_y(0, h)
+
+        round_x(1, 1, share_with_scalar=False)
+        quantize_and_multiply(1, 0, 1)
+        products(1, 1, 0)
+        round_y(False, 0, 0)
+        round_x(1, 2, share_with_scalar=False)
+        quantize_and_multiply(1, 0, 2)
+        round_y(False, 1, 0)
+        round_y(True, 0, 1)
+        round_x(1, 0, share_with_scalar=True)
+        for g_done, g in zip(blocks(0), blocks(1)):
+            quantize_y(g_done, 0)
+            quantize_x(g, 0)
+            product(g, 0, 0)
+        products(1, 1, 1)
+        quantize_y(0, 1)
+        round_y(True, 1, 1)
+        round_x(1, 3, share_with_scalar=True)
+        quantize_y(1, 1)
+        store_words(0)
+        quantize_and_multiply(1, 1, 2)
+
+        first, second = blocks(1)
+        empty_bank(True, first, 0)
+        empty_bank(False, second, 0)
         store_y(1, 0)
-        evacuate(True, 0, 1)
-        evacuate(True, 1, 1)
+        empty_bank(False, first, 1)
+        empty_bank(True, second, 1)
         store_y(1, 1)
-        il(False, 2, 1)
-        il(False, 3, 1)
-        quant_x(2, 1)
-        tap(2, 0, 1, True, False)
-        tap(2, 1, 0, True, False)
-        quant_x(3, 1)
-        tap(3, 0, 1, True, False)
-        tap(3, 1, 0, True, False)
-        oil(False, 0, 0)
-        il(False, 2, 2)
-        il(False, 3, 2)
-        quant_x(2, 2)
-        tap(2, 0, 2, False, False)
-        quant_x(3, 2)
-        tap(3, 0, 2, False, False)
-        tap(2, 1, 1, False, False)
-        tap(3, 1, 1, False, False)
-        oil(True, 1, 0)
-        oil(True, 0, 1)
-        quant_y(0, 0)
-        il(False, 2, 0)
-        il(False, 3, 0)
-        quant_x(2, 0)
-        tap(2, 0, 0, False, True)
-        quant_x(3, 0)
-        tap(3, 0, 0, False, True)
-        quant_y(1, 0)
-        il(False, 2, 3)
-        il(True, 3, 3)
-        oil(False, 1, 1)
-        quant_x(2, 3)
-        tap(2, 1, 2, False, True)
-        quant_y(0, 1)
-        quant_x(3, 3)
-        tap(3, 1, 2, False, True)
-        quant_y(1, 1)
-        store_words(0, 2)
-        evacuate(True, 2, 0)
-        evacuate(False, 3, 0)
-        store_y(3, 0)
-        evacuate(True, 2, 1)
-        oil(False, 2, 0)
-        evacuate(True, 3, 1)
-        store_y(3, 1)
-        oil(False, 3, 0)
-        quant_y(2, 0)
-        oil(False, 2, 1)
-        quant_y(3, 0)
-        oil(False, 3, 1)
-        quant_y(2, 1)
-        quant_y(3, 1)
-        store_words(2, 4)
-        for q in range(4):
-            eng = nc.sync if q % 2 == 0 else nc.scalar
-            eng.dma_start(
+        round_y(False, first, 0)
+        round_y(False, second, 0)
+        round_y(False, first, 1)
+        round_y(True, second, 1)
+        for h in range(HALVES):
+            for g in blocks(1):
+                quantize_y(g, h)
+        store_words(1)
+        for q in range(QUADRANTS):
+            queue = nc.sync if q % 2 == 0 else nc.scalar
+            queue.dma_start(
                 out=out_2[0, 4 * q : 4 * q + 4, :].bitcast(I32),
                 in_=y_sc[32 * q : 32 * q + 4, :].bitcast(I32),
             )

from contextlib import ExitStack

import concourse.mybir as mybir

D, K, M, T = 512, 512, 512, 1024
FLOPS = 3 * 2 * K * M * T

F32 = mybir.dt.float32
BF16 = mybir.dt.bfloat16
I32 = mybir.dt.int32
U32 = mybir.dt.uint32
U8 = mybir.dt.uint8
FP8X4 = mybir.dt.float8_e4m3fn_x4
FP4X4 = mybir.dt.float4_e2m1fn_x4
ACT = mybir.ActivationFunctionType

P = 128
PACK = 4
LINE = 4
QUADRANTS = 4
TAPS = 3
BLOCK = 128
SLAB = 2 * BLOCK
SLABS = D // SLAB
HALVES = T // D
W2_PART = P // 2
WINDOW_ORDER = (1, 2, 0, 3)


def tile_mix_dconv_fm_pl_bias_kernel(
    tc, x, w0_words, w0_scales, w1_words, w1_scales, w2, b, out_0, out_1, out_2
):
    nc = tc.nc
    with ExitStack() as ctx:
        sb = ctx.enter_context(tc.tile_pool(name="sb", bufs=1))
        ps = ctx.enter_context(tc.psum_pool(name="ps", bufs=1))
        ctx.enter_context(tc.manual_schedule())

        def tile(name, shape, dtype):
            return sb.tile(shape, dtype, name=name, align_bytes=64)

        def blocks(slab):
            return (2 * slab, 2 * slab + 1)

        def within_slab(slab_tile, g):
            c0 = BLOCK * (g % 2)
            return slab_tile[:, :, c0 : c0 + BLOCK]

        w0_raw = tile("w0_raw", [P, 2 * M], U8)
        w0_codes = tile("w0_codes", [P, 2 * M], U8)
        w1_raw = tile("w1_raw", [P, M], U32)
        w1_codes = tile("w1_codes", [P, M], U32)
        packed_sc_raw = [tile("packed_sc_raw%d" % s, [P, M], U8) for s in range(2)]
        packed_sc = [tile("packed_sc%d" % s, [P, M], U8) for s in range(2)]
        w2_raw = tile("w2_raw", [P, PACK, M], F32)
        w2_bf = [tile("w2_bf%d" % part, [P, PACK * W2_PART * PACK], BF16) for part in range(2)]
        w2_codes = tile("w2_codes", [P, M], U32)
        w2_sc = tile("w2_sc", [P, M], U8)
        bias = tile("bias", [P, PACK], F32)

        x_loads = [(slab, j) for slab in range(SLABS) for j in WINDOW_ORDER]
        x_raw = {key: tile("x_raw%d_%d" % key, [P, PACK, SLAB], F32) for key in x_loads}
        x_keys = [(g, j) for slab, j in x_loads for g in blocks(slab)]
        x_bf = {key: tile("x_bf%d_%d" % key, [P, PACK * BLOCK], BF16) for key in x_keys}
        x_codes = {key: tile("x_codes%d_%d" % key, [P, BLOCK], U32) for key in x_keys}
        x_sc = {key: tile("x_sc%d_%d" % key, [P, BLOCK], U8) for key in x_keys}

        y_keys = [(g, h) for g in range(2 * SLABS) for h in range(HALVES)]
        acc = {key: ps.tile([P, PACK * BLOCK], F32, name="acc%d_%d" % key) for key in y_keys}
        y = {(slab, h): tile("y%d_%d" % (slab, h), [P, PACK, SLAB], F32) for slab in range(SLABS) for h in range(HALVES)}
        y_bf = {key: tile("y_bf%d_%d" % key, [P, PACK * BLOCK], BF16) for key in y_keys}
        y_codes = tile("y_codes", [P, T], U32)
        y_sc = tile("y_sc", [P, T], U8)

        x_rows = x.rearrange("(p i) t -> p i t", i=PACK)
        out_rows = out_0.rearrange("(p r) t -> p r t", r=PACK)
        out_words = out_1[0].rearrange("p t i -> p (t i)").bitcast(I32)

        def load_x(slab, j):
            c0 = D * j + SLAB * slab
            nc.sync.dma_start(out=x_raw[slab, j][:], in_=x_rows[:, :, c0 : c0 + SLAB])

        def load_scales(s, src):
            for q in range(QUADRANTS):
                nc.sync.dma_start(
                    out=packed_sc_raw[s][32 * q : 32 * q + 4, :].bitcast(I32),
                    in_=src[0, 4 * q : 4 * q + 4, :].bitcast(I32),
                )

        def round_to_bf16(on_scalar, out, in_):
            if on_scalar:
                nc.scalar.activation(out=out, in_=in_, func=ACT.Copy)
            else:
                nc.vector.tensor_copy(out=out, in_=in_)

        def interleave(on_scalar, dst, src):
            round_to_bf16(
                on_scalar,
                dst[:].rearrange("p (c e i) -> p c i e", e=LINE, i=PACK),
                src.rearrange("p i (c e) -> p c i e", e=LINE),
            )

        def deal_w0():
            nc.vector.tensor_copy(
                out=w0_codes[:].rearrange("p (r m e) -> p r m e", r=PACK, e=2),
                in_=w0_raw[:].rearrange("p (m r e) -> p r m e", r=PACK, e=2),
            )

        def deal_w1():
            nc.vector.tensor_copy(
                out=w1_codes[:].bitcast(I32).rearrange("p (r a e) -> p a r e", r=PACK, e=LINE),
                in_=w1_raw[:].bitcast(I32).rearrange("p (a e r) -> p a r e", r=PACK, e=LINE),
            )

        def deal_scales(s):
            nc.vector.tensor_copy(
                out=packed_sc[s][:].rearrange("p (r m) -> p r m", r=PACK),
                in_=packed_sc_raw[s][:].rearrange("p (m r) -> p r m", r=PACK),
            )

        def round_w2(on_scalar, part):
            round_to_bf16(
                on_scalar,
                w2_bf[part][:].rearrange("p (r m i) -> p m r i", r=PACK, i=PACK),
                w2_raw[:, :, part * M // 2 : (part + 1) * M // 2].rearrange("p i (m r) -> p m r i", r=PACK),
            )

        def quantize_w2(part):
            for r in range(PACK):
                c0 = P * r + W2_PART * part
                nc.vector.quantize_mx(
                    out=w2_codes[:, c0 : c0 + W2_PART].bitcast(FP8X4),
                    scales=w2_sc[:, c0 : c0 + W2_PART],
                    in_=w2_bf[part][:, PACK * W2_PART * r : PACK * W2_PART * (r + 1)],
                )

        def round_x(slab, j, share_with_scalar):
            first, second = blocks(slab)
            interleave(False, x_bf[first, j], within_slab(x_raw[slab, j], first))
            interleave(share_with_scalar, x_bf[second, j], within_slab(x_raw[slab, j], second))

        def quantize_x(g, j):
            nc.vector.quantize_mx(out=x_codes[g, j][:].bitcast(FP8X4), scales=x_sc[g, j][:], in_=x_bf[g, j][:])

        def product(g, h, s):
            j = h + s
            for r in range(PACK):
                cols = slice(P * r, P * (r + 1))
                if s == 0:
                    lhsT = w0_codes[:, 2 * P * r : 2 * P * (r + 1)].bitcast(FP4X4)
                    lhsT_scale = packed_sc[0][:, cols]
                elif s == 1:
                    lhsT = w1_codes[:, cols].bitcast(FP8X4)
                    lhsT_scale = packed_sc[1][:, cols]
                else:
                    lhsT = w2_codes[:, cols].bitcast(FP8X4)
                    lhsT_scale = w2_sc[:, cols]
                nc.tensor.matmul_mx(
                    out=acc[g, h][:, BLOCK * r : BLOCK * (r + 1)],
                    lhsT=lhsT,
                    lhsT_scale=lhsT_scale,
                    rhs=x_codes[g, j][:].bitcast(FP8X4),
                    rhs_scale=x_sc[g, j][:],
                    start=(j == WINDOW_ORDER[0] and r == 0),
                    stop=(j == TAPS * h and r == PACK - 1),
                )

        def products(slab, h, s):
            for g in blocks(slab):
                product(g, h, s)

        def quantize_and_multiply(slab, h, s):
            for g in blocks(slab):
                quantize_x(g, h + s)
                product(g, h, s)

        def empty_bank(on_scalar, g, h):
            dst = within_slab(y[g // 2, h], g)
            if on_scalar:
                for r in range(PACK):
                    nc.scalar.activation(
                        out=dst[:, r, :],
                        in_=acc[g, h][:, BLOCK * r : BLOCK * (r + 1)],
                        func=ACT.Identity,
                        bias=bias[:, r : r + 1],
                    )
            else:
                nc.vector.tensor_tensor(
                    out=dst,
                    in0=acc[g, h][:].rearrange("p (r c) -> p r c", r=PACK),
                    in1=bias[:].unsqueeze(2).to_broadcast([P, PACK, BLOCK]),
                    op=mybir.AluOpType.add,
                )

        def round_y(on_scalar, g, h):
            interleave(on_scalar, y_bf[g, h], within_slab(y[g // 2, h], g))

        def quantize_y(g, h):
            c0 = D * h + BLOCK * g
            nc.vector.quantize_mx(
                out=y_codes[:, c0 : c0 + BLOCK].bitcast(FP8X4), scales=y_sc[:, c0 : c0 + BLOCK], in_=y_bf[g, h][:]
            )

        def store_y(slab, h):
            c0 = D * h + SLAB * slab
            nc.sync.dma_start(out=out_rows[:, :, c0 : c0 + SLAB], in_=y[slab, h][:])

        def store_words(slab):
            cols = slice(SLAB * slab, SLAB * (slab + 1))
            nc.sync.dma_start(
                out=out_words.rearrange("p (h t) -> p h t", h=HALVES)[:, :, cols],
                in_=y_codes[:].bitcast(I32).rearrange("p (h t) -> p h t", h=HALVES)[:, :, cols],
            )

        nc.vector.memset(packed_sc_raw[1][:].bitcast(I32), 0)
        nc.vector.memset(packed_sc_raw[0][:].bitcast(I32), 0)
        load_x(*x_loads[0])
        load_scales(1, w1_scales)
        nc.sync.dma_start(out=w1_raw[:].bitcast(I32), in_=w1_words[0].rearrange("p n i -> p (n i)").bitcast(I32))
        nc.sync.dma_start(out=w0_raw[:].bitcast(I32), in_=w0_words[0].bitcast(I32))
        nc.sync.dma_start(out=w2_raw[:], in_=w2.rearrange("(p i) n -> p i n", i=PACK))
        load_scales(0, w0_scales)
        load_x(*x_loads[1])
        nc.sync.dma_start(out=bias[:], in_=b.rearrange("(p r) -> p r", r=PACK))
        for key in x_loads[2:]:
            load_x(*key)

        round_x(0, 1, share_with_scalar=True)
        deal_scales(1)
        deal_w1()
        quantize_and_multiply(0, 0, 1)
        deal_w0()
        round_w2(True, 0)
        round_w2(False, 1)
        deal_scales(0)
        products(0, 1, 0)
        quantize_w2(1)
        round_x(0, 2, share_with_scalar=True)
        quantize_w2(0)
        quantize_and_multiply(0, 0, 2)
        round_x(0, 0, share_with_scalar=True)
        quantize_and_multiply(0, 0, 0)
        products(0, 1, 1)
        round_x(0, 3, share_with_scalar=False)
        quantize_and_multiply(0, 1, 2)
        for h in range(HALVES):
            for g in blocks(0):
                empty_bank(True, g, h)
            store_y(0, h)

        round_x(1, 1, share_with_scalar=False)
        quantize_and_multiply(1, 0, 1)
        products(1, 1, 0)
        round_y(False, 0, 0)
        round_x(1, 2, share_with_scalar=False)
        quantize_and_multiply(1, 0, 2)
        round_y(False, 1, 0)
        round_y(True, 0, 1)
        round_x(1, 0, share_with_scalar=True)
        for g_done, g in zip(blocks(0), blocks(1)):
            quantize_y(g_done, 0)
            quantize_x(g, 0)
            product(g, 0, 0)
        products(1, 1, 1)
        quantize_y(0, 1)
        round_y(True, 1, 1)
        round_x(1, 3, share_with_scalar=True)
        quantize_y(1, 1)
        store_words(0)
        quantize_and_multiply(1, 1, 2)

        first, second = blocks(1)
        empty_bank(True, first, 0)
        empty_bank(False, second, 0)
        store_y(1, 0)
        empty_bank(False, first, 1)
        empty_bank(True, second, 1)
        store_y(1, 1)
        round_y(False, first, 0)
        round_y(False, second, 0)
        round_y(False, first, 1)
        round_y(True, second, 1)
        for h in range(HALVES):
            for g in blocks(1):
                quantize_y(g, h)
        store_words(1)
        for q in range(QUADRANTS):
            queue = nc.sync if q % 2 == 0 else nc.scalar
            queue.dma_start(
                out=out_2[0, 4 * q : 4 * q + 4, :].bitcast(I32),
                in_=y_sc[32 * q : 32 * q + 4, :].bitcast(I32),
            )
